import numpy as np, ml_dtypes
CORES = [16,32,48,64,80]
N = 5
import mx_ref
KO = 2
F = np.float32(1.3)
OWN = [3,3,3,3,3]
BF = ml_dtypes.bfloat16
def tile(rs):
    return np.stack(rs, axis=2).reshape(128, -1).astype(BF)
def pick(b):
    s = np.zeros((128, 128, 4), np.float32)
    s[np.arange(128), np.arange(128), b] = 1.0
    return mx_ref.quantize(s.reshape(128, 512).astype(BF))
def pk(c, s, i=0):
    return (np.ascontiguousarray(c[:, 512 * i:512 * i + 512]), mx_ref.live(s[:, 128 * i:128 * i + 128]))
def inputs(rng, e, E):
    def f(*shape):
        v = (rng.standard_normal(shape, dtype=np.float32) * np.exp2(rng.integers(-2, 3, shape[:-1] + (1,)))).astype(BF)
        return mx_ref.spread((v.astype(np.float32) * np.exp2(rng.integers(-E, E + 1, shape[:-2] + (1, 1))).astype(np.float32)).astype(BF), rng, e)
    def packed(k):
        c = np.zeros((N, 128, k * 512), np.uint8); s = np.zeros((N, 128, k * 128), np.uint8)
        for r in range(N):
            for i in range(k):
                a, b = mx_ref.quantize(f(128, 512)); c[r][:, 512 * i:512 * i + 512] = a; s[r][:, 128 * i:128 * i + 128] = mx_ref.plane(b, rng)
        return c, s
    d = {}
    d["kc"], d["ks"] = packed(KO)
    d["q"] = f(N, 128, 512)
    return d
def setup_inputs(rng):
    return inputs(rng, 0, 0)
def setup_inputs_blocks(rng):
    return inputs(rng, 4, 0)
def setup_inputs_wide(rng):
    return inputs(rng, 0, 8)
def reference(kc, ks, q):
    S = [pick(t) for t in range(4)]
    anew = lambda p, i: mx_ref.quantize(tile([mx_ref.matmul(S[t], pk(kc[p], ks[p], i)) * F for t in range(4)]))
    y = np.full((N, 128, 1280), np.nan, np.float32)
    for o in range(N):
        if OWN[o] != o: continue
        qq = mx_ref.quantize(q[o])
        M = [pk(kc[o], ks[o], i) for i in range(KO)] + [anew(p, i) for p in range(N) if p != o and OWN[p] == o for i in range(KO)]
        y[o][:, :128 * len(M)] = np.concatenate([mx_ref.matmul(qq, m) for m in M], axis=1)
    return {"y": y}

@@ -1,0 +1,137 @@
+import numpy as np
+from concourse.mybir import dt, AluOpType, ActivationFunctionType
+
+W = 128
+KO = 2
+BANK = 512
+BANKS = 8
+FACTOR = float(np.float32(1.3))
+
+SCRATCH = {
+    "c_in": ("sbuf", [128, KO * W], "float8_e4m3fn_x4"),
+    "s_in": ("sbuf", [128, KO * W], "uint8"),
+    "q_in": ("sbuf", [128, 4 * W], "bfloat16"),
+    "q_c": ("sbuf", [128, W], "float8_e4m3fn_x4"),
+    "q_s": ("sbuf", [128, W], "uint8"),
+    "land_c": ("sbuf", [128, 4 * KO * W], "float8_e4m3fn_x4"),
+    "land_s": ("sbuf", [128, 4 * KO * W], "uint8"),
+    "out": ("sbuf", [128, 1280], "float32"),
+    "diff": ("sbuf", [128, W], "bfloat16"),
+    "sel": ("sbuf", [128, 4 * W + 4], "bfloat16"),
+    "sel_c": ("sbuf", [128, 4 * W], "float8_e4m3fn_x4"),
+    "sel_s": ("sbuf", [128, 4 * W], "uint8"),
+    "new0": ("sbuf", [128, 4 * W], "bfloat16"),
+    "new1": ("sbuf", [128, 4 * W], "bfloat16"),
+    "new_c": ("sbuf", [128, KO * W], "float8_e4m3fn_x4"),
+    "new_s": ("sbuf", [128, KO * W], "uint8"),
+    "ps": ("psum", [128, BANK * BANKS], "float32"),
+}
+SEMAPHORES = (["ld_c0", "ld_c1", "ld_s", "ld_q", "zero", "diag", "sel_q", "q_q", "new_q0", "new_q1", "sent", "stored"]
+              + ["mm%d" % j for j in range(9)] + ["ev%d" % j for j in range(9)]
+              + ["a0_%d" % p for p in range(4)] + ["a1_%d" % p for p in range(4)])
+
+
+def codes(buf, a, b):
+    return buf[:, a:b].bitcast(dt.uint8)
+
+
+def producer(g, core, dst, slot, T, topo):
+    g.sync.dma_start(codes(T.c_in, 0, W), T.kc[:, 0:4 * W]).then_inc(T.sem.ld_c0, 16)
+    g.scalar.dma_start(T.s_in[:], T.ks[:]).then_inc(T.sem.ld_s, 16)
+    g.sync.dma_start(codes(T.c_in, W, 2 * W), T.kc[:, 4 * W:8 * W]).then_inc(T.sem.ld_c1, 16)
+
+    g.iota(T.diff[:], [[-1, W]], 0, 1, allow_small_or_imprecise_dtypes=True).then_inc(T.sem.zero, 1)
+    g.vector.memset(T.sel[:], 0.0).then_inc(T.sem.zero, 1)
+    g.vector.wait_ge(T.sem.zero, 2)
+    g.vector.tensor_scalar(T.sel[:, 3:4 * W + 3:4], T.diff[:], 0.0, None, AluOpType.is_equal).then_inc(T.sem.diag, 1)
+    g.vector.wait_ge(T.sem.diag, 1)
+    for b in range(4):
+        g.vector.quantize_mx(T.sel_c[:, b * W:(b + 1) * W], T.sel_s[:, b * W:(b + 1) * W],
+                             T.sel[:, 3 - b:3 - b + 4 * W]).then_inc(T.sem.sel_q, 1)
+
+    g.tensor.wait_ge(T.sem.sel_q, 4)
+    g.tensor.wait_ge(T.sem.ld_s, 16)
+    for i in range(KO):
+        g.tensor.wait_ge(T.sem["ld_c%d" % i], 16)
+        for b in range(4):
+            j = 4 * i + b
+            g.tensor.matmul_mx(T.ps[:, BANK * j:BANK * j + W], T.sel_c[:, b * W:(b + 1) * W], T.sel_s[:, b * W:(b + 1) * W],
+                               T.c_in[:, i * W:(i + 1) * W], T.s_in[:, i * W:(i + 1) * W], True, True).then_inc(T.sem["mm%d" % j], 1)
+
+    for i in range(KO):
+        new = T["new%d" % i]
+        for b in range(4):
+            j = 4 * i + b
+            src = T.ps[:, BANK * j:BANK * j + W]
+            to = new[:, b:4 * W:4]
+            if b % 2 == 0:
+                g.vector.wait_ge(T.sem["mm%d" % j], 1)
+                g.vector.tensor_scalar(to, src, FACTOR, None, AluOpType.mult).then_inc(T.sem["ev%d" % i], 1)
+            else:
+                g.scalar.wait_ge(T.sem["mm%d" % j], 1)
+                g.scalar.activation(to, src, ActivationFunctionType.Copy, scale=FACTOR).then_inc(T.sem["ev%d" % i], 1)
+        g.vector.wait_ge(T.sem["ev%d" % i], 4)
+        g.vector.quantize_mx(T.new_c[:, i * W:(i + 1) * W], T.new_s[:, i * W:(i + 1) * W], new[:]).then_inc(T.sem["new_q%d" % i], 1)
+
+    rid, pid, _ = topo.addr(dst)
+    eng = topo.mask(core, dst)
+    at = slot * KO * W
+    a0, a1 = T.sem["a0_%d" % slot], T.sem["a1_%d" % slot]
+    g.wait_ge(T.sem.new_q0, 1)
+    g.remote_dma(codes(T.land_c, at, at + W), codes(T.new_c, 0, W), a0, T.sem.sent, pid, rid, eng)
+    g.wait_ge(T.sem.new_q1, 1)
+    g.remote_dma(T.land_s[:, at:at + KO * W], T.new_s[:], a0, T.sem.sent, pid, rid, eng)
+    g.remote_dma(codes(T.land_c, at + W, at + 2 * W), codes(T.new_c, W, 2 * W), a1, T.sem.sent, pid, rid, eng)
+    g.wait_ge(T.sem.sent, 3 * bin(eng).count("1"))
+
+
+def consumer(g, core, sources, T, topo):
+    g.sync.dma_start(T.q_in[:], T.q[:]).then_inc(T.sem.ld_q, 16)
+    g.scalar.dma_start(T.s_in[:], T.ks[:]).then_inc(T.sem.ld_s, 16)
+    g.sync.dma_start(codes(T.c_in, 0, KO * W), T.kc[:]).then_inc(T.sem.ld_c0, 16)
+    g.vector.wait_ge(T.sem.ld_q, 16)
+    g.vector.quantize_mx(T.q_c[:], T.q_s[:], T.q_in[:]).then_inc(T.sem.q_q, 1)
+    g.tensor.wait_ge(T.sem.q_q, 1)
+
+    jobs = [([(T.sem.ld_s, 16), (T.sem.ld_c0, 16)], T.c_in, T.s_in, 0, 0, KO * W)]
+    for i in range(KO):
+        for slot, src in enumerate(sources):
+            n = bin(topo.mask(src, core)).count("1")
+            waits = [(T.sem["a0_%d" % slot], 2 * n)] if i == 0 else [(T.sem["a1_%d" % slot], n)]
+            at = (slot * KO + i) * W
+            jobs.append((waits, T.land_c, T.land_s, at, KO * W + at, W))
+
+    last = len(jobs) - 1
+    for j, (waits, c, s, at, col, n) in enumerate(jobs):
+        bank = BANK * (j % BANKS)
+        if j >= BANKS:
+            g.tensor.wait_ge(T.sem["ev%d" % (j - BANKS)], 1)
+        for sem, val in waits:
+            g.tensor.wait_ge(sem, val)
+        g.tensor.matmul_mx(T.ps[:, bank:bank + n], T.q_c[:], T.q_s[:], c[:, at:at + n], s[:, at:at + n],
+                           True, True).then_inc(T.sem["mm%d" % j], 1)
+        src, to = T.ps[:, bank:bank + n], T.out[:, col:col + n]
+        mm, ev = T.sem["mm%d" % j], T.sem["ev%d" % j]
+        if j % 2 == 1 or j == 0:
+            g.vector.wait_ge(mm, 1)
+            g.vector.tensor_copy(to, src).then_inc(ev, 1)
+        else:
+            g.scalar.wait_ge(mm, 1)
+            g.scalar.activation(to, src, ActivationFunctionType.Copy).then_inc(ev, 1)
+        q = g.scalar if j == last else g.sync
+        q.wait_ge(ev, 1)
+        q.dma_start(T.y[:, col:col + n], to).then_inc(T.sem.stored, 16)
+    g.sync.wait_ge(T.sem.stored, 16 * len(jobs))
+
+
+def rank_program(g, core, T, topo):
+    rank = T.rank_of(core)
+    if rank is None:
+        return
+    own = T.tables["OWN"]
+    o = own[rank]
+    sources = [p for p in range(len(own)) if p != o and own[p] == o]
+    if o == rank:
+        consumer(g, core, [T.cores[p] for p in sources], T, topo)
+    else:
+        producer(g, core, T.cores[o], sources.index(rank), T, topo)

@@ -1,11 +1,14 @@
 import numpy as np
 from concourse.mybir import dt, AluOpType, ActivationFunctionType
 
+SIM_CORES = 96
 W = 128
 KO = 2
 BANK = 512
 BANKS = 8
 FACTOR = float(np.float32(1.3))
+RELAYED = 2
+RUN = 96
 
 SCRATCH = {
     "c_in": ("sbuf", [128, KO * W], "float8_e4m3fn_x4"),
@@ -24,15 +27,25 @@ SCRATCH = {
     "new1": ("sbuf", [128, 4 * W], "bfloat16"),
     "new_c": ("sbuf", [128, KO * W], "float8_e4m3fn_x4"),
     "new_s": ("sbuf", [128, KO * W], "uint8"),
+    "hop": ("sbuf", [128, RUN], "float8_e4m3fn_x4"),
     "ps": ("psum", [128, BANK * BANKS], "float32"),
 }
-SEMAPHORES = (["ld_c0", "ld_c1", "ld_s", "ld_q", "zero", "diag", "sel_q", "q_q", "new_q0", "new_q1", "sent", "stored"]
-              + ["mm%d" % j for j in range(9)] + ["ev%d" % j for j in range(9)]
-              + ["a0_%d" % p for p in range(4)] + ["a1_%d" % p for p in range(4)])
+SEMAPHORES = (["ld_c0", "ld_c1", "ld_s", "ld_q", "zero", "diag", "q_q", "new_q0", "new_q1", "sent", "stored", "hop_in"]
+              + ["sel_q%d" % b for b in range(4)] + ["mm%d" % j for j in range(9)] + ["ev%d" % j for j in range(9)]
+              + ["as_%d" % p for p in range(4)] + ["a0_%d" % p for p in range(4)] + ["a1_%d" % p for p in range(4)])
 
 
 def codes(buf, a, b):
     return buf[:, a:b].bitcast(dt.uint8)
+
+
+def count(eng):
+    return bin(eng).count("1")
+
+
+def helper_of(core, dst, topo):
+    return [c for c in range(SIM_CORES) if topo.chip(c) == topo.chip(core) and topo.die(c) != topo.die(dst)
+            and topo.may_write(c, dst)][0]
 
 
 def producer(g, core, dst, slot, T, topo):
@@ -47,13 +60,14 @@ def producer(g, core, dst, slot, T, topo):
     g.vector.wait_ge(T.sem.diag, 1)
     for b in range(4):
         g.vector.quantize_mx(T.sel_c[:, b * W:(b + 1) * W], T.sel_s[:, b * W:(b + 1) * W],
-                             T.sel[:, 3 - b:3 - b + 4 * W]).then_inc(T.sem.sel_q, 1)
+                             T.sel[:, 3 - b:3 - b + 4 * W]).then_inc(T.sem["sel_q%d" % b], 1)
 
-    g.tensor.wait_ge(T.sem.sel_q, 4)
     g.tensor.wait_ge(T.sem.ld_s, 16)
     for i in range(KO):
         g.tensor.wait_ge(T.sem["ld_c%d" % i], 16)
         for b in range(4):
+            if i == 0:
+                g.tensor.wait_ge(T.sem["sel_q%d" % b], 1)
             j = 4 * i + b
             g.tensor.matmul_mx(T.ps[:, BANK * j:BANK * j + W], T.sel_c[:, b * W:(b + 1) * W], T.sel_s[:, b * W:(b + 1) * W],
                                T.c_in[:, i * W:(i + 1) * W], T.s_in[:, i * W:(i + 1) * W], True, True).then_inc(T.sem["mm%d" % j], 1)
@@ -64,7 +78,7 @@ def producer(g, core, dst, slot, T, topo):
             j = 4 * i + b
             src = T.ps[:, BANK * j:BANK * j + W]
             to = new[:, b:4 * W:4]
-            if b % 2 == 0:
+            if b % 2 == 1:
                 g.vector.wait_ge(T.sem["mm%d" % j], 1)
                 g.vector.tensor_scalar(to, src, FACTOR, None, AluOpType.mult).then_inc(T.sem["ev%d" % i], 1)
             else:
@@ -76,13 +90,30 @@ def producer(g, core, dst, slot, T, topo):
     rid, pid, _ = topo.addr(dst)
     eng = topo.mask(core, dst)
     at = slot * KO * W
-    a0, a1 = T.sem["a0_%d" % slot], T.sem["a1_%d" % slot]
     g.wait_ge(T.sem.new_q0, 1)
-    g.remote_dma(codes(T.land_c, at, at + W), codes(T.new_c, 0, W), a0, T.sem.sent, pid, rid, eng)
+    if slot < RELAYED:
+        h = helper_of(core, dst, topo)
+        hrid, hpid, _ = topo.addr(h)
+        first = topo.mask(core, h) & eng
+        g.remote_dma(codes(T.hop, 0, RUN), codes(T.new_c, 0, RUN), T.sem.hop_in, T.sem.sent, hpid, hrid, first)
+        begin = RUN
+    else:
+        first = eng
+        g.remote_dma(codes(T.land_c, at, at + W), codes(T.new_c, 0, W), T.sem["a0_%d" % slot], T.sem.sent, pid, rid, first)
+        begin = W
     g.wait_ge(T.sem.new_q1, 1)
-    g.remote_dma(T.land_s[:, at:at + KO * W], T.new_s[:], a0, T.sem.sent, pid, rid, eng)
-    g.remote_dma(codes(T.land_c, at + W, at + 2 * W), codes(T.new_c, W, 2 * W), a1, T.sem.sent, pid, rid, eng)
-    g.wait_ge(T.sem.sent, 3 * bin(eng).count("1"))
+    g.remote_dma(T.land_s[:, at:at + KO * W], T.new_s[:], T.sem["as_%d" % slot], T.sem.sent, pid, rid, eng)
+    g.remote_dma(codes(T.land_c, at + begin, at + 2 * W), codes(T.new_c, begin, 2 * W), T.sem["a1_%d" % slot], T.sem.sent, pid, rid, eng)
+    g.wait_ge(T.sem.sent, count(first) + 2 * count(eng))
+
+
+def helper(g, core, src, dst, slot, T, topo):
+    rid, pid, _ = topo.addr(dst)
+    eng = topo.mask(core, dst)
+    at = slot * KO * W
+    g.wait_ge(T.sem.hop_in, count(topo.mask(src, core) & topo.mask(src, dst)))
+    g.remote_dma(codes(T.land_c, at, at + RUN), codes(T.hop, 0, RUN), T.sem["a0_%d" % slot], T.sem.sent, pid, rid, eng)
+    g.wait_ge(T.sem.sent, count(eng))
 
 
 def consumer(g, core, sources, T, topo):
@@ -94,12 +125,19 @@ def consumer(g, core, sources, T, topo):
     g.tensor.wait_ge(T.sem.q_q, 1)
 
     jobs = [([(T.sem.ld_s, 16), (T.sem.ld_c0, 16)], T.c_in, T.s_in, 0, 0, KO * W)]
-    for i in range(KO):
-        for slot, src in enumerate(sources):
-            n = bin(topo.mask(src, core)).count("1")
-            waits = [(T.sem["a0_%d" % slot], 2 * n)] if i == 0 else [(T.sem["a1_%d" % slot], n)]
-            at = (slot * KO + i) * W
-            jobs.append((waits, T.land_c, T.land_s, at, KO * W + at, W))
+    n_src = len(sources)
+    order = ([(0, p) for p in range(RELAYED, n_src)] + [(1, p) for p in range(RELAYED)]
+             + [(1, p) for p in range(RELAYED, n_src)] + [(0, p) for p in range(RELAYED)])
+    planes_in = set()
+    for i, slot in order:
+        src = sources[slot]
+        via = helper_of(src, core, topo) if i == 0 and slot < RELAYED else src
+        waits = [(T.sem["a%d_%d" % (i, slot)], count(topo.mask(via, core)))]
+        if slot not in planes_in:
+            planes_in.add(slot)
+            waits = [(T.sem["as_%d" % slot], count(topo.mask(src, core)))] + waits
+        at = (slot * KO + i) * W
+        jobs.append((waits, T.land_c, T.land_s, at, KO * W + at, W))
 
     last = len(jobs) - 1
     for j, (waits, c, s, at, col, n) in enumerate(jobs):
@@ -125,13 +163,16 @@ def consumer(g, core, sources, T, topo):
 
 
 def rank_program(g, core, T, topo):
-    rank = T.rank_of(core)
-    if rank is None:
-        return
     own = T.tables["OWN"]
-    o = own[rank]
-    sources = [p for p in range(len(own)) if p != o and own[p] == o]
-    if o == rank:
-        consumer(g, core, [T.cores[p] for p in sources], T, topo)
-    else:
-        producer(g, core, T.cores[o], sources.index(rank), T, topo)
+    for o in range(len(own)):
+        if own[o] != o:
+            continue
+        dst = T.cores[o]
+        sources = [T.cores[p] for p in range(len(own)) if p != o and own[p] == o]
+        if core == dst:
+            consumer(g, core, sources, T, topo)
+        for slot, src in enumerate(sources):
+            if core == src:
+                producer(g, core, dst, slot, T, topo)
+            elif slot < RELAYED and core == helper_of(src, dst, topo):
+                helper(g, core, src, dst, slot, T, topo)

import numpy as np
from concourse.mybir import dt, AluOpType, ActivationFunctionType

SIM_CORES = 96
W = 128
KO = 2
BANK = 512
BANKS = 8
FACTOR = float(np.float32(1.3))
RELAYED = 2
RUN = 96

SCRATCH = {
    "c_in": ("sbuf", [128, KO * W], "float8_e4m3fn_x4"),
    "s_in": ("sbuf", [128, KO * W], "uint8"),
    "q_in": ("sbuf", [128, 4 * W], "bfloat16"),
    "q_c": ("sbuf", [128, W], "float8_e4m3fn_x4"),
    "q_s": ("sbuf", [128, W], "uint8"),
    "land_c": ("sbuf", [128, 4 * KO * W], "float8_e4m3fn_x4"),
    "land_s": ("sbuf", [128, 4 * KO * W], "uint8"),
    "out": ("sbuf", [128, 1280], "float32"),
    "diff": ("sbuf", [128, W], "bfloat16"),
    "sel": ("sbuf", [128, 4 * W + 4], "bfloat16"),
    "sel_c": ("sbuf", [128, 4 * W], "float8_e4m3fn_x4"),
    "sel_s": ("sbuf", [128, 4 * W], "uint8"),
    "new0": ("sbuf", [128, 4 * W], "bfloat16"),
    "new1": ("sbuf", [128, 4 * W], "bfloat16"),
    "new_c": ("sbuf", [128, KO * W], "float8_e4m3fn_x4"),
    "new_s": ("sbuf", [128, KO * W], "uint8"),
    "hop": ("sbuf", [128, RUN], "float8_e4m3fn_x4"),
    "ps": ("psum", [128, BANK * BANKS], "float32"),
}
SEMAPHORES = (["ld_c0", "ld_c1", "ld_s", "ld_q", "zero", "diag", "q_q", "new_q0", "new_q1", "sent", "stored", "hop_in"]
              + ["sel_q%d" % b for b in range(4)] + ["mm%d" % j for j in range(9)] + ["ev%d" % j for j in range(9)]
              + ["as_%d" % p for p in range(4)] + ["a0_%d" % p for p in range(4)] + ["a1_%d" % p for p in range(4)])


def codes(buf, a, b):
    return buf[:, a:b].bitcast(dt.uint8)


def count(eng):
    return bin(eng).count("1")


def helper_of(core, dst, topo):
    return [c for c in range(SIM_CORES) if topo.chip(c) == topo.chip(core) and topo.die(c) != topo.die(dst)
            and topo.may_write(c, dst)][0]


def producer(g, core, dst, slot, T, topo):
    g.sync.dma_start(codes(T.c_in, 0, W), T.kc[:, 0:4 * W]).then_inc(T.sem.ld_c0, 16)
    g.scalar.dma_start(T.s_in[:], T.ks[:]).then_inc(T.sem.ld_s, 16)
    g.sync.dma_start(codes(T.c_in, W, 2 * W), T.kc[:, 4 * W:8 * W]).then_inc(T.sem.ld_c1, 16)

    g.iota(T.diff[:], [[-1, W]], 0, 1, allow_small_or_imprecise_dtypes=True).then_inc(T.sem.zero, 1)
    g.vector.memset(T.sel[:], 0.0).then_inc(T.sem.zero, 1)
    g.vector.wait_ge(T.sem.zero, 2)
    g.vector.tensor_scalar(T.sel[:, 3:4 * W + 3:4], T.diff[:], 0.0, None, AluOpType.is_equal).then_inc(T.sem.diag, 1)
    g.vector.wait_ge(T.sem.diag, 1)
    for b in range(4):
        g.vector.quantize_mx(T.sel_c[:, b * W:(b + 1) * W], T.sel_s[:, b * W:(b + 1) * W],
                             T.sel[:, 3 - b:3 - b + 4 * W]).then_inc(T.sem["sel_q%d" % b], 1)

    g.tensor.wait_ge(T.sem.ld_s, 16)
    for i in range(KO):
        g.tensor.wait_ge(T.sem["ld_c%d" % i], 16)
        for b in range(4):
            if i == 0:
                g.tensor.wait_ge(T.sem["sel_q%d" % b], 1)
            j = 4 * i + b
            g.tensor.matmul_mx(T.ps[:, BANK * j:BANK * j + W], T.sel_c[:, b * W:(b + 1) * W], T.sel_s[:, b * W:(b + 1) * W],
                               T.c_in[:, i * W:(i + 1) * W], T.s_in[:, i * W:(i + 1) * W], True, True).then_inc(T.sem["mm%d" % j], 1)

    for i in range(KO):
        new = T["new%d" % i]
        for b in range(4):
            j = 4 * i + b
            src = T.ps[:, BANK * j:BANK * j + W]
            to = new[:, b:4 * W:4]
            if b % 2 == 1:
                g.vector.wait_ge(T.sem["mm%d" % j], 1)
                g.vector.tensor_scalar(to, src, FACTOR, None, AluOpType.mult).then_inc(T.sem["ev%d" % i], 1)
            else:
                g.scalar.wait_ge(T.sem["mm%d" % j], 1)
                g.scalar.activation(to, src, ActivationFunctionType.Copy, scale=FACTOR).then_inc(T.sem["ev%d" % i], 1)
        g.vector.wait_ge(T.sem["ev%d" % i], 4)
        g.vector.quantize_mx(T.new_c[:, i * W:(i + 1) * W], T.new_s[:, i * W:(i + 1) * W], new[:]).then_inc(T.sem["new_q%d" % i], 1)

    rid, pid, _ = topo.addr(dst)
    eng = topo.mask(core, dst)
    at = slot * KO * W
    g.wait_ge(T.sem.new_q0, 1)
    if slot < RELAYED:
        h = helper_of(core, dst, topo)
        hrid, hpid, _ = topo.addr(h)
        first = topo.mask(core, h) & eng
        g.remote_dma(codes(T.hop, 0, RUN), codes(T.new_c, 0, RUN), T.sem.hop_in, T.sem.sent, hpid, hrid, first)
        begin = RUN
    else:
        first = eng
        g.remote_dma(codes(T.land_c, at, at + W), codes(T.new_c, 0, W), T.sem["a0_%d" % slot], T.sem.sent, pid, rid, first)
        begin = W
    g.wait_ge(T.sem.new_q1, 1)
    g.remote_dma(T.land_s[:, at:at + KO * W], T.new_s[:], T.sem["as_%d" % slot], T.sem.sent, pid, rid, eng)
    g.remote_dma(codes(T.land_c, at + begin, at + 2 * W), codes(T.new_c, begin, 2 * W), T.sem["a1_%d" % slot], T.sem.sent, pid, rid, eng)
    g.wait_ge(T.sem.sent, count(first) + 2 * count(eng))


def helper(g, core, src, dst, slot, T, topo):
    rid, pid, _ = topo.addr(dst)
    eng = topo.mask(core, dst)
    at = slot * KO * W
    g.wait_ge(T.sem.hop_in, count(topo.mask(src, core) & topo.mask(src, dst)))
    g.remote_dma(codes(T.land_c, at, at + RUN), codes(T.hop, 0, RUN), T.sem["a0_%d" % slot], T.sem.sent, pid, rid, eng)
    g.wait_ge(T.sem.sent, count(eng))


def consumer(g, core, sources, T, topo):
    g.sync.dma_start(T.q_in[:], T.q[:]).then_inc(T.sem.ld_q, 16)
    g.scalar.dma_start(T.s_in[:], T.ks[:]).then_inc(T.sem.ld_s, 16)
    g.sync.dma_start(codes(T.c_in, 0, KO * W), T.kc[:]).then_inc(T.sem.ld_c0, 16)
    g.vector.wait_ge(T.sem.ld_q, 16)
    g.vector.quantize_mx(T.q_c[:], T.q_s[:], T.q_in[:]).then_inc(T.sem.q_q, 1)
    g.tensor.wait_ge(T.sem.q_q, 1)

    jobs = [([(T.sem.ld_s, 16), (T.sem.ld_c0, 16)], T.c_in, T.s_in, 0, 0, KO * W)]
    n_src = len(sources)
    order = ([(0, p) for p in range(RELAYED, n_src)] + [(1, p) for p in range(RELAYED)]
             + [(1, p) for p in range(RELAYED, n_src)] + [(0, p) for p in range(RELAYED)])
    planes_in = set()
    for i, slot in order:
        src = sources[slot]
        via = helper_of(src, core, topo) if i == 0 and slot < RELAYED else src
        waits = [(T.sem["a%d_%d" % (i, slot)], count(topo.mask(via, core)))]
        if slot not in planes_in:
            planes_in.add(slot)
            waits = [(T.sem["as_%d" % slot], count(topo.mask(src, core)))] + waits
        at = (slot * KO + i) * W
        jobs.append((waits, T.land_c, T.land_s, at, KO * W + at, W))

    last = len(jobs) - 1
    for j, (waits, c, s, at, col, n) in enumerate(jobs):
        bank = BANK * (j % BANKS)
        if j >= BANKS:
            g.tensor.wait_ge(T.sem["ev%d" % (j - BANKS)], 1)
        for sem, val in waits:
            g.tensor.wait_ge(sem, val)
        g.tensor.matmul_mx(T.ps[:, bank:bank + n], T.q_c[:], T.q_s[:], c[:, at:at + n], s[:, at:at + n],
                           True, True).then_inc(T.sem["mm%d" % j], 1)
        src, to = T.ps[:, bank:bank + n], T.out[:, col:col + n]
        mm, ev = T.sem["mm%d" % j], T.sem["ev%d" % j]
        if j % 2 == 1 or j == 0:
            g.vector.wait_ge(mm, 1)
            g.vector.tensor_copy(to, src).then_inc(ev, 1)
        else:
            g.scalar.wait_ge(mm, 1)
            g.scalar.activation(to, src, ActivationFunctionType.Copy).then_inc(ev, 1)
        q = g.scalar if j == last else g.sync
        q.wait_ge(ev, 1)
        q.dma_start(T.y[:, col:col + n], to).then_inc(T.sem.stored, 16)
    g.sync.wait_ge(T.sem.stored, 16 * len(jobs))


def rank_program(g, core, T, topo):
    own = T.tables["OWN"]
    for o in range(len(own)):
        if own[o] != o:
            continue
        dst = T.cores[o]
        sources = [T.cores[p] for p in range(len(own)) if p != o and own[p] == o]
        if core == dst:
            consumer(g, core, sources, T, topo)
        for slot, src in enumerate(sources):
            if core == src:
                producer(g, core, dst, slot, T, topo)
            elif slot < RELAYED and core == helper_of(src, dst, topo):
                helper(g, core, src, dst, slot, T, topo)
